import numpy as np
import ml_dtypes


def mxq(x, axis, fmt="e4m3"):
    dtype, down = {"e4m3": (ml_dtypes.float8_e4m3fn, 7), "e5m2": (ml_dtypes.float8_e5m2, 14)}[fmt]
    v = np.moveaxis(np.asarray(x, np.float32).astype(ml_dtypes.bfloat16).astype(np.float64), axis, -1)
    blocks = v.reshape(v.shape[:-1] + (-1, 32))
    amax = np.abs(blocks).max(-1, keepdims=True)
    byte = np.maximum(np.where(amax > 0, np.frexp(amax)[1] - 1 + 127, 0) - down, 1)
    scale = np.exp2(byte - 127.0)
    codes = (blocks / scale).astype(np.float32).astype(dtype).astype(np.float64)
    return np.moveaxis((codes * scale).reshape(v.shape), -1, axis)


WIDE = False


def mx_kscale(k):
    if not WIDE:
        return np.ones(k)
    levels = np.array([10, -10, 5, -5, 0])
    if k % 512:
        return np.exp2(np.random.permutation(np.resize(levels, k // 32))).repeat(32)
    a = np.empty((k // 512, 16))
    for p in range(k // 512):
        a[p, :8] = np.random.permutation(np.resize(levels, 8))
        for g in range(8):
            far = levels[np.abs(levels - a[p, g]) >= 10]
            a[p, g + 8] = far[np.random.randint(len(far))]
    return np.exp2(a.ravel()).repeat(32)


def f64(x):
    return np.asarray(x).astype(np.float64)


def striped(idx):
    return np.tile(idx.reshape(-1, 16).T, (8, 1)).astype(np.uint16)


def unstriped(offs):
    return offs[:16].T.reshape(-1).astype(np.int64)


def striped8(idx):
    return np.concatenate([x.reshape(-1, 16).T for x in idx]).astype(np.uint16)


def runs(offs, k):
    lists = np.stack([offs[16 * r : 16 * r + 16].T.reshape(-1) for r in range(8)]).astype(np.int64)
    return lists[np.arange(k) % 512 // 64]


def pack_weight(w):
    k, n = w.shape
    w = f64(np.asarray(w, np.float32).astype(ml_dtypes.bfloat16)).reshape(k // 32, 32, n)
    amax = np.abs(w).max(1)
    byte = np.clip(np.where(amax > 0, np.frexp(amax)[1] - 1 + 127 - 7, 1), 1, 254)
    scaled = (w * np.exp2(127.0 - byte)[:, None, :]).reshape(k, n).astype(np.float32)
    words = np.ascontiguousarray(scaled.reshape(k // 512, 128, 4, n).transpose(0, 1, 3, 2)).astype(ml_dtypes.float8_e4m3fn).view(np.uint8)
    return words, np.ascontiguousarray(byte.astype(np.uint8).reshape(k // 512, 16, n))


def unpack_weight(words, scales):
    g, p, n, _ = words.shape
    vals = np.ascontiguousarray(words).view(ml_dtypes.float8_e4m3fn).astype(np.float64) * np.repeat(np.exp2(scales.astype(np.float64) - 127.0), 8, axis=1)[..., None]
    return vals.transpose(0, 1, 3, 2).reshape(g * 512, n)


def relu(v):
    return np.maximum(v, 0.0)


K, T, S, V, H = 512, 2048, 512, 256, 512


def setup_inputs():
    n = np.random.standard_normal
    s = mx_kscale(K)[:, None]
    packed_xT = pack_weight(n((K, T)) * s)
    return {
        "x_words": packed_xT[0],
        "x_scales": packed_xT[1],
        "w1": (n((K, H)) / np.sqrt(K) / s).astype(np.float32),
        "gs": (np.random.uniform(0.5, 1.5, (K, 1)) / s).astype(np.float32),
        "offs": striped(np.random.permutation(T)[:S]),
        "l1": striped8(np.stack([np.random.permutation(S)[:V] for _ in range(8)])),
        "l2": striped8(np.stack([np.random.permutation(S)[:V] for _ in range(8)])),
        "cand": striped(np.random.permutation(T)[:S]),
    }


def reference(x_words, x_scales, w1, gs, offs, l1, l2, cand):
    x_cand = unpack_weight(x_words, x_scales)[:, unstriped(cand)]
    xq = unpack_weight(x_words, x_scales)[:, unstriped(offs)]
    h = relu(mxq(f64(w1), 0, "e4m3").T @ xq)
    z = f64(gs) * (h[np.arange(H)[:, None], runs(l1, H)] - (h[np.arange(H)[:, None], runs(l2, H)]))
    return 0.0625 * ((x_cand.T @ mxq(z, 0, "e4m3")))

@@ -1,0 +1,162 @@
+from contextlib import ExitStack
+
+import concourse.mybir as mybir
+
+K, T, S, V, H = 512, 2048, 512, 256, 512
+FLOPS = 2 * K * H * S + 2 * K * S * V
+
+F32 = mybir.dt.float32
+BF16 = mybir.dt.bfloat16
+I32 = mybir.dt.int32
+U32 = mybir.dt.uint32
+U16 = mybir.dt.uint16
+U8 = mybir.dt.uint8
+FP8X4 = mybir.dt.float8_e4m3fn_x4
+COPY = mybir.ActivationFunctionType.Copy
+RELU = mybir.ActivationFunctionType.Relu
+MULT = mybir.AluOpType.mult
+SUB = mybir.AluOpType.subtract
+
+P = 128
+PACK = 4
+HALF_V = V // 2
+OUT_SCALE = 0.0625
+
+
+def tile_picked_candpair8_none_p_kernel(
+    tc, x_words, x_scales, w1, gs, offs, l1, l2, cand, out
+):
+    nc = tc.nc
+    with ExitStack() as ctx:
+        keep = ctx.enter_context(tc.tile_pool(name="keep", bufs=1))
+        psum = ctx.enter_context(tc.psum_pool(name="psum", bufs=1))
+
+        offs_t = keep.tile([P, S // 16], U16, name="offs_t")
+        cand_t = keep.tile([P, S // 16], U16, name="cand_t")
+        l1_t = keep.tile([P, V // 16], U16, name="l1_t")
+        l2_t = keep.tile([P, V // 16], U16, name="l2_t")
+        scale_win = keep.tile([P, T], U8, name="scale_win")
+        word_win = keep.tile([P, T], U32, name="word_win")
+        w_raw = [keep.tile([P, PACK, H // 2], F32, name="w_raw%d" % u) for u in range(2)]
+        gs_t = keep.tile([P, PACK], F32, name="gs_t")
+
+        nc.vector.memset(scale_win[:].bitcast(I32), 0)
+        nc.sync.dma_start(offs_t[:], offs)
+        nc.sync.dma_start(cand_t[:], cand)
+        for q in range(4):
+            nc.sync.dma_start(
+                scale_win[32 * q : 32 * q + 4, :].bitcast(I32),
+                x_scales[0, 4 * q : 4 * q + 4, :].bitcast(I32),
+            )
+        w_rows = w1.rearrange("(p j) c -> p j c", j=PACK)
+        for u in range(2):
+            nc.sync.dma_start(w_raw[u][:], w_rows[:, :, u * (H // 2) : (u + 1) * (H // 2)])
+        nc.sync.dma_start(
+            word_win[:].bitcast(I32), x_words[0].rearrange("p n t -> p (n t)").bitcast(I32)
+        )
+        nc.sync.dma_start(l2_t[:], l2)
+        nc.sync.dma_start(l1_t[:], l1)
+        nc.sync.dma_start(gs_t[:], gs.rearrange("(p t) o -> p (t o)", t=PACK))
+
+        xq_s = keep.tile([P, S], U8, name="xq_s", align_bytes=64)
+        xc_s = keep.tile([P, S], U8, name="xc_s", align_bytes=64)
+        nc.vector.tensor_copy(xq_s[:], scale_win[:].indirect(offs_t[:]))
+        nc.vector.tensor_copy(xc_s[:], scale_win[:].indirect(cand_t[:]))
+
+        w_grp = keep.tile([P, PACK * H], BF16, name="w_grp", align_bytes=64)
+        w_dst = w_grp[:].rearrange("p (t m j) -> p m t j", t=PACK, j=PACK)
+        w_src = [w_raw[u][:].rearrange("p j (m t) -> p m t j", t=PACK) for u in range(2)]
+        nc.scalar.activation(w_dst[:, 0:64], w_src[0], COPY)
+        nc.scalar.activation(w_dst[:, 64:96], w_src[1][:, 0:32], COPY)
+        nc.vector.tensor_copy(w_dst[:, 96:128], w_src[1][:, 32:64])
+        w_codes = keep.tile([P, H], U32, name="w_codes", align_bytes=64)
+        w_s = keep.tile([P, H], U8, name="w_s", align_bytes=64)
+        nc.vector.quantize_mx(out=w_codes[:].bitcast(FP8X4), scales=w_s[:], in_=w_grp[:])
+
+        xq_w = keep.tile([P, S], U32, name="xq_w", align_bytes=64)
+        xc_w = keep.tile([P, S], U32, name="xc_w", align_bytes=64)
+        for u in range(2):
+            nc.vector.tensor_copy(
+                xq_w[:, u * 256 : (u + 1) * 256], word_win[:].indirect(offs_t[:, u * 16 : (u + 1) * 16])
+            )
+        nc.vector.tensor_copy(xc_w[:], word_win[:].indirect(cand_t[:]))
+
+        h = []
+        for t in range(PACK):
+            bank = psum.tile([P, S], F32, name="h_bank%d" % t)
+            cols = slice(t * P, (t + 1) * P)
+            for u in range(2):
+                toks = slice(u * 256, (u + 1) * 256)
+                nc.tensor.matmul_mx(
+                    out=bank[:, toks],
+                    lhsT=w_codes[:, cols].bitcast(FP8X4),
+                    lhsT_scale=w_s[:, cols],
+                    rhs=xq_w[:, toks].bitcast(FP8X4),
+                    rhs_scale=xq_s[:, toks],
+                    start=True,
+                    stop=True,
+                )
+            h_t = keep.tile([P, S], F32, name="h%d" % t)
+            nc.scalar.activation(h_t[:], bank[:], RELU)
+            h.append(h_t)
+
+        z_planes = [keep.tile([P, PACK, HALF_V], BF16, name="z_planes%d" % u) for u in range(2)]
+
+        def pairs(lst, u):
+            return lst[:, u * (HALF_V // 16) : (u + 1) * (HALF_V // 16)]
+
+        def fetch(jobs, second, diff):
+            for i, (t, u) in enumerate(jobs):
+                nc.vector.tensor_copy(second[:, i, :], h[t][:].indirect(pairs(l2_t, u)))
+            for i, (t, u) in enumerate(jobs):
+                nc.vector.tensor_tensor(diff[:, i, :], h[t][:].indirect(pairs(l1_t, u)), second[:, i, :], SUB)
+            for i, (t, u) in enumerate(jobs):
+                nc.scalar.activation(z_planes[u][:, t, :], diff[:, i, :], COPY, scale=gs_t[:, t : t + 1])
+
+        def finish(u):
+            z_grp = keep.tile([P, HALF_V * PACK], BF16, name="z_grp%d" % u, align_bytes=64)
+            dst = z_grp[:].rearrange("p (c i t) -> p c t i", i=4, t=PACK)
+            src = z_planes[u][:].rearrange("p t (c i) -> p c t i", i=4)
+            if u == 0:
+                nc.scalar.copy(dst, src)
+            else:
+                nc.vector.tensor_copy(dst, src)
+            z_codes = keep.tile([P, HALF_V], U32, name="z_codes%d" % u, align_bytes=64)
+            z_s = keep.tile([P, HALF_V], U8, name="z_s%d" % u, align_bytes=64)
+            nc.vector.quantize_mx(out=z_codes[:].bitcast(FP8X4), scales=z_s[:], in_=z_grp[:])
+            groups = [range(0, 4)] if u == 0 else [range(0, 2), range(2, 4)]
+            out_rows = out.rearrange("(c p) v -> p c v", p=P)
+            for g, blocks in enumerate(groups):
+                bank = psum.tile([P, len(blocks), HALF_V], F32, name="o_bank%d_%d" % (u, g))
+                for i, c in enumerate(blocks):
+                    cols = slice(c * P, (c + 1) * P)
+                    nc.tensor.matmul_mx(
+                        out=bank[:, i, :],
+                        lhsT=xc_w[:, cols].bitcast(FP8X4),
+                        lhsT_scale=xc_s[:, cols],
+                        rhs=z_codes[:].bitcast(FP8X4),
+                        rhs_scale=z_s[:],
+                        start=True,
+                        stop=True,
+                    )
+                res = keep.tile([P, len(blocks), HALF_V], F32, name="res%d_%d" % (u, g))
+                dest = out_rows[:, blocks.start : blocks.stop, u * HALF_V : (u + 1) * HALF_V]
+                if u == 1 and g == 0:
+                    nc.vector.tensor_scalar(res[:], bank[:], OUT_SCALE, None, op0=MULT)
+                    nc.sync.dma_start(dest, res[:])
+                elif u == 1:
+                    nc.scalar.activation(res[:], bank[:], COPY, scale=OUT_SCALE)
+                    nc.scalar.dma_start(dest, res[:])
+                else:
+                    nc.scalar.activation(res[:], bank[:], COPY, scale=OUT_SCALE)
+                    nc.sync.dma_start(dest, res[:])
+
+        for t in range(2):
+            second = keep.tile([P, 2, HALF_V], F32, name="second%d" % t)
+            diff = keep.tile([P, 2, HALF_V], F32, name="diff%d" % t, tag="shared%d" % t)
+            fetch([(t, 0), (t, 1)], second, diff)
+        for u in range(2):
+            second = keep.tile([P, 2, HALF_V], F32, name="late_second%d" % u, tag="shared%d" % u)
+            diff = keep.tile([P, 2, HALF_V], F32, name="late_diff%d" % u)
+            fetch([(2, u), (3, u)], second, diff)
+            finish(u)

@@ -37,20 +37,21 @@ def tile_picked_candpair8_none_p_kernel(
         l2_t = keep.tile([P, V // 16], U16, name="l2_t")
         scale_win = keep.tile([P, T], U8, name="scale_win")
         word_win = keep.tile([P, T], U32, name="word_win")
-        w_raw = [keep.tile([P, PACK, H // 2], F32, name="w_raw%d" % u) for u in range(2)]
+        w_first = keep.tile([P, PACK, 128], F32, name="w_first")
+        w_rest = keep.tile([P, PACK, H - 128], F32, name="w_rest")
         gs_t = keep.tile([P, PACK], F32, name="gs_t")
 
         nc.vector.memset(scale_win[:].bitcast(I32), 0)
         nc.sync.dma_start(offs_t[:], offs)
-        nc.sync.dma_start(cand_t[:], cand)
+        w_rows = w1.rearrange("(p j) c -> p j c", j=PACK)
+        nc.sync.dma_start(w_first[:], w_rows[:, :, 0:128])
         for q in range(4):
             nc.sync.dma_start(
                 scale_win[32 * q : 32 * q + 4, :].bitcast(I32),
                 x_scales[0, 4 * q : 4 * q + 4, :].bitcast(I32),
             )
-        w_rows = w1.rearrange("(p j) c -> p j c", j=PACK)
-        for u in range(2):
-            nc.sync.dma_start(w_raw[u][:], w_rows[:, :, u * (H // 2) : (u + 1) * (H // 2)])
+        nc.sync.dma_start(cand_t[:], cand)
+        nc.sync.dma_start(w_rest[:], w_rows[:, :, 128:H])
         nc.sync.dma_start(
             word_win[:].bitcast(I32), x_words[0].rearrange("p n t -> p (n t)").bitcast(I32)
         )
@@ -65,10 +66,10 @@ def tile_picked_candpair8_none_p_kernel(
 
         w_grp = keep.tile([P, PACK * H], BF16, name="w_grp", align_bytes=64)
         w_dst = w_grp[:].rearrange("p (t m j) -> p m t j", t=PACK, j=PACK)
-        w_src = [w_raw[u][:].rearrange("p j (m t) -> p m t j", t=PACK) for u in range(2)]
-        nc.scalar.activation(w_dst[:, 0:64], w_src[0], COPY)
-        nc.scalar.activation(w_dst[:, 64:96], w_src[1][:, 0:32], COPY)
-        nc.vector.tensor_copy(w_dst[:, 96:128], w_src[1][:, 32:64])
+        w_src = [w[:].rearrange("p j (m t) -> p m t j", t=PACK) for w in (w_first, w_rest)]
+        nc.scalar.activation(w_dst[:, 0:32], w_src[0], COPY)
+        nc.scalar.activation(w_dst[:, 32:88], w_src[1][:, 0:56], COPY)
+        nc.vector.tensor_copy(w_dst[:, 88:128], w_src[1][:, 56:96])
         w_codes = keep.tile([P, H], U32, name="w_codes", align_bytes=64)
         w_s = keep.tile([P, H], U8, name="w_s", align_bytes=64)
         nc.vector.quantize_mx(out=w_codes[:].bitcast(FP8X4), scales=w_s[:], in_=w_grp[:])
@@ -85,8 +86,7 @@ def tile_picked_candpair8_none_p_kernel(
         for t in range(PACK):
             bank = psum.tile([P, S], F32, name="h_bank%d" % t)
             cols = slice(t * P, (t + 1) * P)
-            for u in range(2):
-                toks = slice(u * 256, (u + 1) * 256)
+            for toks in [slice(0, 256), slice(256, 512)] if t == 0 else [slice(0, 512)]:
                 nc.tensor.matmul_mx(
                     out=bank[:, toks],
                     lhsT=w_codes[:, cols].bitcast(FP8X4),
@@ -100,36 +100,32 @@ def tile_picked_candpair8_none_p_kernel(
             nc.scalar.activation(h_t[:], bank[:], RELU)
             h.append(h_t)
 
-        z_planes = [keep.tile([P, PACK, HALF_V], BF16, name="z_planes%d" % u) for u in range(2)]
+        z_grp = [keep.tile([P, HALF_V, PACK], BF16, name="z_grp%d" % u, align_bytes=64) for u in range(2)]
 
         def pairs(lst, u):
             return lst[:, u * (HALF_V // 16) : (u + 1) * (HALF_V // 16)]
 
-        def fetch(jobs, second, diff):
-            for i, (t, u) in enumerate(jobs):
-                nc.vector.tensor_copy(second[:, i, :], h[t][:].indirect(pairs(l2_t, u)))
-            for i, (t, u) in enumerate(jobs):
-                nc.vector.tensor_tensor(diff[:, i, :], h[t][:].indirect(pairs(l1_t, u)), second[:, i, :], SUB)
-            for i, (t, u) in enumerate(jobs):
-                nc.scalar.activation(z_planes[u][:, t, :], diff[:, i, :], COPY, scale=gs_t[:, t : t + 1])
+        for t in range(PACK):
+            second = keep.tile([P, 2, HALF_V], F32, name="second%d" % t)
+            diff = keep.tile([P, 2, HALF_V], F32, name="diff%d" % t)
+            for u in range(2):
+                nc.vector.tensor_copy(second[:, u, :], h[t][:].indirect(pairs(l2_t, u)))
+            for u in range(2):
+                nc.vector.tensor_tensor(diff[:, u, :], h[t][:].indirect(pairs(l1_t, u)), second[:, u, :], SUB)
+            for u in range(2):
+                nc.scalar.activation(z_grp[u][:, :, t], diff[:, u, :], COPY, scale=gs_t[:, t : t + 1])
 
-        def finish(u):
-            z_grp = keep.tile([P, HALF_V * PACK], BF16, name="z_grp%d" % u, align_bytes=64)
-            dst = z_grp[:].rearrange("p (c i t) -> p c t i", i=4, t=PACK)
-            src = z_planes[u][:].rearrange("p t (c i) -> p c t i", i=4)
-            if u == 0:
-                nc.scalar.copy(dst, src)
-            else:
-                nc.vector.tensor_copy(dst, src)
+        out_rows = out.rearrange("(c p) v -> p c v", p=P)
+        for u in range(2):
             z_codes = keep.tile([P, HALF_V], U32, name="z_codes%d" % u, align_bytes=64)
             z_s = keep.tile([P, HALF_V], U8, name="z_s%d" % u, align_bytes=64)
-            nc.vector.quantize_mx(out=z_codes[:].bitcast(FP8X4), scales=z_s[:], in_=z_grp[:])
-            groups = [range(0, 4)] if u == 0 else [range(0, 2), range(2, 4)]
-            out_rows = out.rearrange("(c p) v -> p c v", p=P)
-            for g, blocks in enumerate(groups):
-                bank = psum.tile([P, len(blocks), HALF_V], F32, name="o_bank%d_%d" % (u, g))
-                for i, c in enumerate(blocks):
-                    cols = slice(c * P, (c + 1) * P)
+            nc.vector.quantize_mx(
+                out=z_codes[:].bitcast(FP8X4), scales=z_s[:], in_=z_grp[u][:].rearrange("p v t -> p (v t)")
+            )
+            for g in range(2):
+                bank = psum.tile([P, 2, HALF_V], F32, name="o_bank%d_%d" % (u, g))
+                for i in range(2):
+                    cols = slice((2 * g + i) * P, (2 * g + i + 1) * P)
                     nc.tensor.matmul_mx(
                         out=bank[:, i, :],
                         lhsT=xc_w[:, cols].bitcast(FP8X4),
@@ -139,24 +135,11 @@ def tile_picked_candpair8_none_p_kernel(
                         start=True,
                         stop=True,
                     )
-                res = keep.tile([P, len(blocks), HALF_V], F32, name="res%d_%d" % (u, g))
-                dest = out_rows[:, blocks.start : blocks.stop, u * HALF_V : (u + 1) * HALF_V]
-                if u == 1 and g == 0:
+                res = keep.tile([P, 2, HALF_V], F32, name="res%d_%d" % (u, g))
+                dest = out_rows[:, 2 * g : 2 * g + 2, u * HALF_V : (u + 1) * HALF_V]
+                if g == 0:
                     nc.vector.tensor_scalar(res[:], bank[:], OUT_SCALE, None, op0=MULT)
                     nc.sync.dma_start(dest, res[:])
-                elif u == 1:
-                    nc.scalar.activation(res[:], bank[:], COPY, scale=OUT_SCALE)
-                    nc.scalar.dma_start(dest, res[:])
                 else:
                     nc.scalar.activation(res[:], bank[:], COPY, scale=OUT_SCALE)
-                    nc.sync.dma_start(dest, res[:])
-
-        for t in range(2):
-            second = keep.tile([P, 2, HALF_V], F32, name="second%d" % t)
-            diff = keep.tile([P, 2, HALF_V], F32, name="diff%d" % t, tag="shared%d" % t)
-            fetch([(t, 0), (t, 1)], second, diff)
-        for u in range(2):
-            second = keep.tile([P, 2, HALF_V], F32, name="late_second%d" % u, tag="shared%d" % u)
-            diff = keep.tile([P, 2, HALF_V], F32, name="late_diff%d" % u)
-            fetch([(2, u), (3, u)], second, diff)
-            finish(u)
+                    nc.scalar.dma_start(dest, res[:])

@@ -37,21 +37,20 @@ def tile_picked_candpair8_none_p_kernel(
         l2_t = keep.tile([P, V // 16], U16, name="l2_t")
         scale_win = keep.tile([P, T], U8, name="scale_win")
         word_win = keep.tile([P, T], U32, name="word_win")
-        w_first = keep.tile([P, PACK, 128], F32, name="w_first")
-        w_rest = keep.tile([P, PACK, H - 128], F32, name="w_rest")
+        w_raw = keep.tile([P, PACK, H], F32, name="w_raw")
         gs_t = keep.tile([P, PACK], F32, name="gs_t")
 
         nc.vector.memset(scale_win[:].bitcast(I32), 0)
         nc.sync.dma_start(offs_t[:], offs)
         w_rows = w1.rearrange("(p j) c -> p j c", j=PACK)
-        nc.sync.dma_start(w_first[:], w_rows[:, :, 0:128])
+        nc.sync.dma_start(w_raw[:, 0:1, :], w_rows[:, 0:1, :])
         for q in range(4):
             nc.sync.dma_start(
                 scale_win[32 * q : 32 * q + 4, :].bitcast(I32),
                 x_scales[0, 4 * q : 4 * q + 4, :].bitcast(I32),
             )
         nc.sync.dma_start(cand_t[:], cand)
-        nc.sync.dma_start(w_rest[:], w_rows[:, :, 128:H])
+        nc.sync.dma_start(w_raw[:, 1:PACK, :], w_rows[:, 1:PACK, :])
         nc.sync.dma_start(
             word_win[:].bitcast(I32), x_words[0].rearrange("p n t -> p (n t)").bitcast(I32)
         )
@@ -66,10 +65,9 @@ def tile_picked_candpair8_none_p_kernel(
 
         w_grp = keep.tile([P, PACK * H], BF16, name="w_grp", align_bytes=64)
         w_dst = w_grp[:].rearrange("p (t m j) -> p m t j", t=PACK, j=PACK)
-        w_src = [w[:].rearrange("p j (m t) -> p m t j", t=PACK) for w in (w_first, w_rest)]
-        nc.scalar.activation(w_dst[:, 0:32], w_src[0], COPY)
-        nc.scalar.activation(w_dst[:, 32:88], w_src[1][:, 0:56], COPY)
-        nc.vector.tensor_copy(w_dst[:, 88:128], w_src[1][:, 56:96])
+        w_src = w_raw[:].rearrange("p j (m t) -> p m t j", t=PACK)
+        nc.scalar.activation(w_dst[:, 0:64], w_src[:, 0:64], COPY)
+        nc.vector.tensor_copy(w_dst[:, 64:128], w_src[:, 64:128])
         w_codes = keep.tile([P, H], U32, name="w_codes", align_bytes=64)
         w_s = keep.tile([P, H], U8, name="w_s", align_bytes=64)
         nc.vector.quantize_mx(out=w_codes[:].bitcast(FP8X4), scales=w_s[:], in_=w_grp[:])

@@ -66,8 +66,9 @@ def tile_picked_candpair8_none_p_kernel(
         w_grp = keep.tile([P, PACK * H], BF16, name="w_grp", align_bytes=64)
         w_dst = w_grp[:].rearrange("p (t m j) -> p m t j", t=PACK, j=PACK)
         w_src = w_raw[:].rearrange("p j (m t) -> p m t j", t=PACK)
-        nc.scalar.activation(w_dst[:, 0:64], w_src[:, 0:64], COPY)
-        nc.vector.tensor_copy(w_dst[:, 64:128], w_src[:, 64:128])
+        nc.scalar.activation(w_dst[:, 0:80, :, 0:1], w_src[:, 0:80, :, 0:1], COPY)
+        nc.scalar.activation(w_dst[:, 0:80, :, 1:PACK], w_src[:, 0:80, :, 1:PACK], COPY)
+        nc.vector.tensor_copy(w_dst[:, 80:128], w_src[:, 80:128])
         w_codes = keep.tile([P, H], U32, name="w_codes", align_bytes=64)
         w_s = keep.tile([P, H], U8, name="w_s", align_bytes=64)
         nc.vector.quantize_mx(out=w_codes[:].bitcast(FP8X4), scales=w_s[:], in_=w_grp[:])
@@ -103,15 +104,24 @@ def tile_picked_candpair8_none_p_kernel(
         def pairs(lst, u):
             return lst[:, u * (HALF_V // 16) : (u + 1) * (HALF_V // 16)]
 
+        seconds = {}
+
+        def subtract(t, u):
+            if u == 0:
+                diff = keep.tile([P, HALF_V], F32, name="diff_a%d" % t)
+            else:
+                diff = keep.tile([P, HALF_V], F32, name="diff_b", bufs=2)
+            nc.vector.tensor_tensor(diff[:], h[t][:].indirect(pairs(l1_t, u)), seconds[t][:, u, :], SUB)
+            nc.scalar.activation(z_grp[u][:, :, t], diff[:], COPY, scale=gs_t[:, t : t + 1])
+
         for t in range(PACK):
-            second = keep.tile([P, 2, HALF_V], F32, name="second%d" % t)
-            diff = keep.tile([P, 2, HALF_V], F32, name="diff%d" % t)
+            seconds[t] = keep.tile([P, 2, HALF_V], F32, name="second%d" % t)
             for u in range(2):
-                nc.vector.tensor_copy(second[:, u, :], h[t][:].indirect(pairs(l2_t, u)))
-            for u in range(2):
-                nc.vector.tensor_tensor(diff[:, u, :], h[t][:].indirect(pairs(l1_t, u)), second[:, u, :], SUB)
-            for u in range(2):
-                nc.scalar.activation(z_grp[u][:, :, t], diff[:, u, :], COPY, scale=gs_t[:, t : t + 1])
+                nc.vector.tensor_copy(seconds[t][:, u, :], h[t][:].indirect(pairs(l2_t, u)))
+            subtract(t, 0)
+            if t > 0:
+                subtract(t - 1, 1)
+        subtract(PACK - 1, 1)
 
         out_rows = out.rearrange("(c p) v -> p c v", p=P)
         for u in range(2):

@@ -83,11 +83,12 @@ def tile_picked_candpair8_none_p_kernel(
 
         h = []
         for t in range(PACK):
-            bank = psum.tile([P, S], F32, name="h_bank%d" % t)
             cols = slice(t * P, (t + 1) * P)
-            for toks in [slice(0, 256), slice(256, 512)] if t == 0 else [slice(0, 512)]:
+            h_t = keep.tile([P, S], F32, name="h%d" % t)
+            for i, toks in enumerate([slice(0, 256), slice(256, 512)] if t == 0 else [slice(0, 512)]):
+                bank = psum.tile([P, toks.stop - toks.start], F32, name="h_bank%d_%d" % (t, i))
                 nc.tensor.matmul_mx(
-                    out=bank[:, toks],
+                    out=bank[:],
                     lhsT=w_codes[:, cols].bitcast(FP8X4),
                     lhsT_scale=w_s[:, cols],
                     rhs=xq_w[:, toks].bitcast(FP8X4),
@@ -95,8 +96,7 @@ def tile_picked_candpair8_none_p_kernel(
                     start=True,
                     stop=True,
                 )
-            h_t = keep.tile([P, S], F32, name="h%d" % t)
-            nc.scalar.activation(h_t[:], bank[:], RELU)
+                nc.scalar.activation(h_t[:, toks], bank[:], RELU)
             h.append(h_t)
 
         z_grp = [keep.tile([P, HALF_V, PACK], BF16, name="z_grp%d" % u, align_bytes=64) for u in range(2)]
@@ -131,7 +131,7 @@ def tile_picked_candpair8_none_p_kernel(
                 out=z_codes[:].bitcast(FP8X4), scales=z_s[:], in_=z_grp[u][:].rearrange("p v t -> p (v t)")
             )
             for g in range(2):
-                bank = psum.tile([P, 2, HALF_V], F32, name="o_bank%d_%d" % (u, g))
+                bank = psum.tile([P, 2, HALF_V], F32, name="o_bank%d_%d" % (u, g), tag="h_bank%d_0" % (2 * u + g))
                 for i in range(2):
                     cols = slice((2 * g + i) * P, (2 * g + i + 1) * P)
                     nc.tensor.matmul_mx(

from contextlib import ExitStack

import concourse.mybir as mybir

K, T, S, V, H = 512, 2048, 512, 256, 512
FLOPS = 2 * K * H * S + 2 * K * S * V

F32 = mybir.dt.float32
BF16 = mybir.dt.bfloat16
I32 = mybir.dt.int32
U32 = mybir.dt.uint32
U16 = mybir.dt.uint16
U8 = mybir.dt.uint8
FP8X4 = mybir.dt.float8_e4m3fn_x4
COPY = mybir.ActivationFunctionType.Copy
RELU = mybir.ActivationFunctionType.Relu
MULT = mybir.AluOpType.mult
SUB = mybir.AluOpType.subtract

P = 128
PACK = 4
HALF_V = V // 2
OUT_SCALE = 0.0625


def tile_picked_candpair8_none_p_kernel(
    tc, x_words, x_scales, w1, gs, offs, l1, l2, cand, out
):
    nc = tc.nc
    with ExitStack() as ctx:
        keep = ctx.enter_context(tc.tile_pool(name="keep", bufs=1))
        psum = ctx.enter_context(tc.psum_pool(name="psum", bufs=1))

        offs_t = keep.tile([P, S // 16], U16, name="offs_t")
        cand_t = keep.tile([P, S // 16], U16, name="cand_t")
        l1_t = keep.tile([P, V // 16], U16, name="l1_t")
        l2_t = keep.tile([P, V // 16], U16, name="l2_t")
        scale_win = keep.tile([P, T], U8, name="scale_win")
        word_win = keep.tile([P, T], U32, name="word_win")
        w_raw = keep.tile([P, PACK, H], F32, name="w_raw")
        gs_t = keep.tile([P, PACK], F32, name="gs_t")

        nc.vector.memset(scale_win[:].bitcast(I32), 0)
        nc.sync.dma_start(offs_t[:], offs)
        w_rows = w1.rearrange("(p j) c -> p j c", j=PACK)
        nc.sync.dma_start(w_raw[:, 0:1, :], w_rows[:, 0:1, :])
        for q in range(4):
            nc.sync.dma_start(
                scale_win[32 * q : 32 * q + 4, :].bitcast(I32),
                x_scales[0, 4 * q : 4 * q + 4, :].bitcast(I32),
            )
        nc.sync.dma_start(cand_t[:], cand)
        nc.sync.dma_start(w_raw[:, 1:PACK, :], w_rows[:, 1:PACK, :])
        nc.sync.dma_start(
            word_win[:].bitcast(I32), x_words[0].rearrange("p n t -> p (n t)").bitcast(I32)
        )
        nc.sync.dma_start(l2_t[:], l2)
        nc.sync.dma_start(l1_t[:], l1)
        nc.sync.dma_start(gs_t[:], gs.rearrange("(p t) o -> p (t o)", t=PACK))

        xq_s = keep.tile([P, S], U8, name="xq_s", align_bytes=64)
        xc_s = keep.tile([P, S], U8, name="xc_s", align_bytes=64)
        nc.vector.tensor_copy(xq_s[:], scale_win[:].indirect(offs_t[:]))
        nc.vector.tensor_copy(xc_s[:], scale_win[:].indirect(cand_t[:]))

        w_grp = keep.tile([P, PACK * H], BF16, name="w_grp", align_bytes=64)
        w_dst = w_grp[:].rearrange("p (t m j) -> p m t j", t=PACK, j=PACK)
        w_src = w_raw[:].rearrange("p j (m t) -> p m t j", t=PACK)
        nc.scalar.activation(w_dst[:, 0:80, :, 0:1], w_src[:, 0:80, :, 0:1], COPY)
        nc.scalar.activation(w_dst[:, 0:80, :, 1:PACK], w_src[:, 0:80, :, 1:PACK], COPY)
        nc.vector.tensor_copy(w_dst[:, 80:128], w_src[:, 80:128])
        w_codes = keep.tile([P, H], U32, name="w_codes", align_bytes=64)
        w_s = keep.tile([P, H], U8, name="w_s", align_bytes=64)
        nc.vector.quantize_mx(out=w_codes[:].bitcast(FP8X4), scales=w_s[:], in_=w_grp[:])

        xq_w = keep.tile([P, S], U32, name="xq_w", align_bytes=64)
        xc_w = keep.tile([P, S], U32, name="xc_w", align_bytes=64)
        for u in range(2):
            nc.vector.tensor_copy(
                xq_w[:, u * 256 : (u + 1) * 256], word_win[:].indirect(offs_t[:, u * 16 : (u + 1) * 16])
            )
        nc.vector.tensor_copy(xc_w[:], word_win[:].indirect(cand_t[:]))

        h = []
        for t in range(PACK):
            cols = slice(t * P, (t + 1) * P)
            h_t = keep.tile([P, S], F32, name="h%d" % t)
            for i, toks in enumerate([slice(0, 256), slice(256, 512)] if t == 0 else [slice(0, 512)]):
                bank = psum.tile([P, toks.stop - toks.start], F32, name="h_bank%d_%d" % (t, i))
                nc.tensor.matmul_mx(
                    out=bank[:],
                    lhsT=w_codes[:, cols].bitcast(FP8X4),
                    lhsT_scale=w_s[:, cols],
                    rhs=xq_w[:, toks].bitcast(FP8X4),
                    rhs_scale=xq_s[:, toks],
                    start=True,
                    stop=True,
                )
                nc.scalar.activation(h_t[:, toks], bank[:], RELU)
            h.append(h_t)

        z_grp = [keep.tile([P, HALF_V, PACK], BF16, name="z_grp%d" % u, align_bytes=64) for u in range(2)]

        def pairs(lst, u):
            return lst[:, u * (HALF_V // 16) : (u + 1) * (HALF_V // 16)]

        seconds = {}

        def subtract(t, u):
            if u == 0:
                diff = keep.tile([P, HALF_V], F32, name="diff_a%d" % t)
            else:
                diff = keep.tile([P, HALF_V], F32, name="diff_b", bufs=2)
            nc.vector.tensor_tensor(diff[:], h[t][:].indirect(pairs(l1_t, u)), seconds[t][:, u, :], SUB)
            nc.scalar.activation(z_grp[u][:, :, t], diff[:], COPY, scale=gs_t[:, t : t + 1])

        for t in range(PACK):
            seconds[t] = keep.tile([P, 2, HALF_V], F32, name="second%d" % t)
            for u in range(2):
                nc.vector.tensor_copy(seconds[t][:, u, :], h[t][:].indirect(pairs(l2_t, u)))
            subtract(t, 0)
            if t > 0:
                subtract(t - 1, 1)
        subtract(PACK - 1, 1)

        out_rows = out.rearrange("(c p) v -> p c v", p=P)
        for u in range(2):
            z_codes = keep.tile([P, HALF_V], U32, name="z_codes%d" % u, align_bytes=64)
            z_s = keep.tile([P, HALF_V], U8, name="z_s%d" % u, align_bytes=64)
            nc.vector.quantize_mx(
                out=z_codes[:].bitcast(FP8X4), scales=z_s[:], in_=z_grp[u][:].rearrange("p v t -> p (v t)")
            )
            for g in range(2):
                bank = psum.tile([P, 2, HALF_V], F32, name="o_bank%d_%d" % (u, g), tag="h_bank%d_0" % (2 * u + g))
                for i in range(2):
                    cols = slice((2 * g + i) * P, (2 * g + i + 1) * P)
                    nc.tensor.matmul_mx(
                        out=bank[:, i, :],
                        lhsT=xc_w[:, cols].bitcast(FP8X4),
                        lhsT_scale=xc_s[:, cols],
                        rhs=z_codes[:].bitcast(FP8X4),
                        rhs_scale=z_s[:],
                        start=True,
                        stop=True,
                    )
                res = keep.tile([P, 2, HALF_V], F32, name="res%d_%d" % (u, g))
                dest = out_rows[:, 2 * g : 2 * g + 2, u * HALF_V : (u + 1) * HALF_V]
                if g == 0:
                    nc.vector.tensor_scalar(res[:], bank[:], OUT_SCALE, None, op0=MULT)
                    nc.sync.dma_start(dest, res[:])
                else:
                    nc.scalar.activation(res[:], bank[:], COPY, scale=OUT_SCALE)
                    nc.scalar.dma_start(dest, res[:])
